import numpy as np
import ml_dtypes


def mxq(x, axis, fmt="e4m3"):
    dtype, down = {"e4m3": (ml_dtypes.float8_e4m3fn, 7), "e5m2": (ml_dtypes.float8_e5m2, 14)}[fmt]
    v = np.moveaxis(np.asarray(x, np.float32).astype(ml_dtypes.bfloat16).astype(np.float64), axis, -1)
    blocks = v.reshape(v.shape[:-1] + (-1, 32))
    amax = np.abs(blocks).max(-1, keepdims=True)
    byte = np.maximum(np.where(amax > 0, np.frexp(amax)[1] - 1 + 127, 0) - down, 1)
    scale = np.exp2(byte - 127.0)
    codes = (blocks / scale).astype(np.float32).astype(dtype).astype(np.float64)
    return np.moveaxis((codes * scale).reshape(v.shape), -1, axis)


WIDE = False


def mx_kscale(k):
    if not WIDE:
        return np.ones(k)
    levels = np.array([10, -10, 5, -5, 0])
    if k % 512:
        return np.exp2(np.random.permutation(np.resize(levels, k // 32))).repeat(32)
    a = np.empty((k // 512, 16))
    for p in range(k // 512):
        a[p, :8] = np.random.permutation(np.resize(levels, 8))
        for g in range(8):
            far = levels[np.abs(levels - a[p, g]) >= 10]
            a[p, g + 8] = far[np.random.randint(len(far))]
    return np.exp2(a.ravel()).repeat(32)


def f64(x):
    return np.asarray(x).astype(np.float64)


def striped8(idx):
    return np.concatenate([v.reshape(-1, 16).T for v in idx]).astype(np.uint16)


def unstriped8(offs):
    return np.stack([offs[16 * g:16 * g + 16].T.reshape(-1) for g in range(8)]).astype(np.int64)


K, M, T, S = 1536, 512, 2048, 512


def setup_inputs():
    n = np.random.standard_normal
    s = mx_kscale(K)[:, None]
    return {
        "xT": (n((K, T)) * s).astype(np.float32),
        "w": (n((K, M)) / np.sqrt(K) / s).astype(np.float32),
        "wgt": np.repeat(np.random.uniform(0.5, 2.0, (8, S)), 16, axis=0).astype(np.float32),
        "r": (n((512, 512))).astype(np.float32),
        "offs": striped8(np.stack([np.random.permutation(T)[:S] for _ in range(8)])),
    }


def reference(xT, w, wgt, r, offs):
    idx = unstriped8(offs)
    group = np.arange(K) % 512 // 64
    xg = f64(wgt)[np.arange(K) // 4 % 128] * f64(xT)[np.arange(K)[:, None], idx[group]]
    xT_ = mxq(xg, 0, "e4m3")
    w_ = mxq(f64(w), 0, "e4m3")
    y = xT_.T @ w_
    return f64(r) + y

@@ -1,0 +1,102 @@
+from contextlib import ExitStack
+
+import concourse.mybir as mybir
+
+K, M, T, S = 1536, 512, 2048, 512
+FLOPS = 2 * K * M * S
+
+F32 = mybir.dt.float32
+BF16 = mybir.dt.bfloat16
+U32 = mybir.dt.uint32
+U16 = mybir.dt.uint16
+U8 = mybir.dt.uint8
+FP8X4 = mybir.dt.float8_e4m3fn_x4
+MULT = mybir.AluOpType.mult
+ADD = mybir.AluOpType.add
+
+P = 128
+PACK = 4
+K_PASS = P * PACK
+PASSES = K // K_PASS
+HALF = S // 2
+W_SCALAR = 192
+
+
+def interleave(copy, out, src):
+    copy(out=out.rearrange("p (c j) -> p c j", j=PACK), in_=src.rearrange("p j c -> p c j"))
+
+
+def tile_list_heads_tm_res_kernel(tc, xT, w, wgt, r, offs, out):
+    nc = tc.nc
+    with ExitStack() as ctx:
+        keep = ctx.enter_context(tc.tile_pool(name="keep", bufs=1))
+        psum = ctx.enter_context(tc.psum_pool(name="psum", bufs=1))
+
+        offsets = keep.tile([P, S // 16], U16, name="offsets")
+        wgt_sb = keep.tile([P, S], F32, name="wgt_sb")
+        x_sb = [[keep.tile([P, T], F32, name=f"x{a}{i}") for i in range(PACK)] for a in range(PASSES)]
+        w_sb = [keep.tile([P, PACK * M], F32, name=f"w{a}") for a in range(PASSES)]
+        r_sb = [keep.tile([P, M], F32, name=f"r{b}") for b in range(S // P)]
+
+        for a in range(PASSES):
+            x_rows = xT[a * K_PASS : (a + 1) * K_PASS, :].rearrange("(p j) t -> p j t", j=PACK)
+            for i in range(PACK):
+                nc.sync.dma_start(out=x_sb[a][i][:], in_=x_rows[:, i, :])
+                if a == 0 and i == 0:
+                    nc.sync.dma_start(offsets[:], offs)
+                    nc.sync.dma_start(out=wgt_sb[:], in_=wgt)
+            nc.sync.dma_start(
+                out=w_sb[a][:],
+                in_=w[a * K_PASS : (a + 1) * K_PASS, :].rearrange("(p j) n -> p (j n)", j=PACK),
+            )
+        for b in range(S // P):
+            nc.sync.dma_start(out=r_sb[b][:], in_=r[b * P : (b + 1) * P, :])
+
+        acc = [psum.tile([P, M], F32, name=f"acc{b}") for b in range(S // P)]
+
+        for a in range(PASSES):
+            last = a == PASSES - 1
+            picked = [keep.tile([P, PACK, HALF], F32, name=f"picked{a}{h}") for h in range(2)]
+            x_bf = [keep.tile([P, HALF * PACK], BF16, name=f"xbf{a}{h}", align_bytes=64) for h in range(2)]
+            x_codes = [keep.tile([P, HALF], U32, name=f"xcodes{a}{h}", align_bytes=64) for h in range(2)]
+            x_scales = [keep.tile([P, HALF], U8, name=f"xscales{a}{h}", align_bytes=64) for h in range(2)]
+            w_bf = keep.tile([P, M * PACK], BF16, name=f"wbf{a}", align_bytes=64)
+            w_codes = keep.tile([P, M], U32, name=f"wcodes{a}", align_bytes=64)
+            w_scales = keep.tile([P, M], U8, name=f"wscales{a}", align_bytes=64)
+
+            for i in range(PACK):
+                for h in range(2):
+                    nc.vector.tensor_tensor(
+                        picked[h][:, i, :],
+                        x_sb[a][i][:].indirect(offsets[:, h * HALF // 16 : (h + 1) * HALF // 16]),
+                        wgt_sb[:, h * HALF : (h + 1) * HALF],
+                        MULT,
+                    )
+            interleave(nc.scalar.copy, x_bf[0][:], picked[0][:])
+            interleave(nc.vector.tensor_copy if last else nc.scalar.copy, x_bf[1][:], picked[1][:])
+            for h in range(2):
+                nc.vector.quantize_mx(out=x_codes[h][:].bitcast(FP8X4), scales=x_scales[h][:], in_=x_bf[h][:])
+
+            w_rows = w_sb[a][:].rearrange("p (j n) -> p j n", j=PACK)
+            split = W_SCALAR if last else M
+            interleave(nc.scalar.copy, w_bf[:, : split * PACK], w_rows[:, :, :split])
+            if last:
+                interleave(nc.vector.tensor_copy, w_bf[:, split * PACK :], w_rows[:, :, split:])
+            nc.vector.quantize_mx(out=w_codes[:].bitcast(FP8X4), scales=w_scales[:], in_=w_bf[:])
+
+            for b in range(S // P):
+                h, cols = b // 2, slice(b % 2 * P, (b % 2 + 1) * P)
+                nc.tensor.matmul_mx(
+                    out=acc[b][:],
+                    lhsT=x_codes[h][:, cols].bitcast(FP8X4),
+                    lhsT_scale=x_scales[h][:, cols],
+                    rhs=w_codes[:].bitcast(FP8X4),
+                    rhs_scale=w_scales[:],
+                    start=a == 0,
+                    stop=last,
+                )
+
+        for b in range(S // P):
+            result = keep.tile([P, M], F32, name=f"result{b}")
+            nc.vector.tensor_tensor(result[:], acc[b][:], r_sb[b][:], ADD)
+            nc.sync.dma_start(out=out[b * P : (b + 1) * P, :], in_=result[:])

@@ -19,7 +19,7 @@ PACK = 4
 K_PASS = P * PACK
 PASSES = K // K_PASS
 HALF = S // 2
-W_SCALAR = 192
+N_HALF = M // 2
 
 
 def interleave(copy, out, src):
@@ -41,10 +41,12 @@ def tile_list_heads_tm_res_kernel(tc, xT, w, wgt, r, offs, out):
         for a in range(PASSES):
             x_rows = xT[a * K_PASS : (a + 1) * K_PASS, :].rearrange("(p j) t -> p j t", j=PACK)
             for i in range(PACK):
-                nc.sync.dma_start(out=x_sb[a][i][:], in_=x_rows[:, i, :])
+                queue = nc.scalar if i % 2 else nc.sync
+                queue.dma_start(out=x_sb[a][i][:], in_=x_rows[:, i, :])
                 if a == 0 and i == 0:
                     nc.sync.dma_start(offsets[:], offs)
                     nc.sync.dma_start(out=wgt_sb[:], in_=wgt)
+        for a in range(PASSES):
             nc.sync.dma_start(
                 out=w_sb[a][:],
                 in_=w[a * K_PASS : (a + 1) * K_PASS, :].rearrange("(p j) n -> p (j n)", j=PACK),
@@ -52,18 +54,14 @@ def tile_list_heads_tm_res_kernel(tc, xT, w, wgt, r, offs, out):
         for b in range(S // P):
             nc.sync.dma_start(out=r_sb[b][:], in_=r[b * P : (b + 1) * P, :])
 
-        acc = [psum.tile([P, M], F32, name=f"acc{b}") for b in range(S // P)]
+        acc = [[psum.tile([P, N_HALF], F32, name=f"acc{b}{g}") for g in range(2)] for b in range(S // P)]
+        x_codes = [[keep.tile([P, HALF], U32, name=f"xcodes{a}{h}", align_bytes=64) for h in range(2)] for a in range(PASSES)]
+        x_scales = [[keep.tile([P, HALF], U8, name=f"xscales{a}{h}", align_bytes=64) for h in range(2)] for a in range(PASSES)]
 
         for a in range(PASSES):
             last = a == PASSES - 1
             picked = [keep.tile([P, PACK, HALF], F32, name=f"picked{a}{h}") for h in range(2)]
             x_bf = [keep.tile([P, HALF * PACK], BF16, name=f"xbf{a}{h}", align_bytes=64) for h in range(2)]
-            x_codes = [keep.tile([P, HALF], U32, name=f"xcodes{a}{h}", align_bytes=64) for h in range(2)]
-            x_scales = [keep.tile([P, HALF], U8, name=f"xscales{a}{h}", align_bytes=64) for h in range(2)]
-            w_bf = keep.tile([P, M * PACK], BF16, name=f"wbf{a}", align_bytes=64)
-            w_codes = keep.tile([P, M], U32, name=f"wcodes{a}", align_bytes=64)
-            w_scales = keep.tile([P, M], U8, name=f"wscales{a}", align_bytes=64)
-
             for i in range(PACK):
                 for h in range(2):
                     nc.vector.tensor_tensor(
@@ -75,28 +73,32 @@ def tile_list_heads_tm_res_kernel(tc, xT, w, wgt, r, offs, out):
             interleave(nc.scalar.copy, x_bf[0][:], picked[0][:])
             interleave(nc.vector.tensor_copy if last else nc.scalar.copy, x_bf[1][:], picked[1][:])
             for h in range(2):
-                nc.vector.quantize_mx(out=x_codes[h][:].bitcast(FP8X4), scales=x_scales[h][:], in_=x_bf[h][:])
+                nc.vector.quantize_mx(out=x_codes[a][h][:].bitcast(FP8X4), scales=x_scales[a][h][:], in_=x_bf[h][:])
 
+        for a in range(PASSES):
             w_rows = w_sb[a][:].rearrange("p (j n) -> p j n", j=PACK)
-            split = W_SCALAR if last else M
-            interleave(nc.scalar.copy, w_bf[:, : split * PACK], w_rows[:, :, :split])
-            if last:
-                interleave(nc.vector.tensor_copy, w_bf[:, split * PACK :], w_rows[:, :, split:])
-            nc.vector.quantize_mx(out=w_codes[:].bitcast(FP8X4), scales=w_scales[:], in_=w_bf[:])
+            w_bf = [keep.tile([P, N_HALF * PACK], BF16, name=f"wbf{a}{g}", align_bytes=64) for g in range(2)]
+            w_codes = [keep.tile([P, N_HALF], U32, name=f"wcodes{a}{g}", align_bytes=64) for g in range(2)]
+            w_scales = [keep.tile([P, N_HALF], U8, name=f"wscales{a}{g}", align_bytes=64) for g in range(2)]
+            for g in range(2):
+                interleave(nc.scalar.copy if g else nc.vector.tensor_copy, w_bf[g][:], w_rows[:, :, g * N_HALF : (g + 1) * N_HALF])
+            for g in range(2):
+                nc.vector.quantize_mx(out=w_codes[g][:].bitcast(FP8X4), scales=w_scales[g][:], in_=w_bf[g][:])
+                for b in range(S // P):
+                    h, cols = b // 2, slice(b % 2 * P, (b % 2 + 1) * P)
+                    nc.tensor.matmul_mx(
+                        out=acc[b][g][:],
+                        lhsT=x_codes[a][h][:, cols].bitcast(FP8X4),
+                        lhsT_scale=x_scales[a][h][:, cols],
+                        rhs=w_codes[g][:].bitcast(FP8X4),
+                        rhs_scale=w_scales[g][:],
+                        start=a == 0,
+                        stop=a == PASSES - 1,
+                    )
 
+        for g in range(2):
+            cols = slice(g * N_HALF, (g + 1) * N_HALF)
             for b in range(S // P):
-                h, cols = b // 2, slice(b % 2 * P, (b % 2 + 1) * P)
-                nc.tensor.matmul_mx(
-                    out=acc[b][:],
-                    lhsT=x_codes[h][:, cols].bitcast(FP8X4),
-                    lhsT_scale=x_scales[h][:, cols],
-                    rhs=w_codes[:].bitcast(FP8X4),
-                    rhs_scale=w_scales[:],
-                    start=a == 0,
-                    stop=last,
-                )
-
-        for b in range(S // P):
-            result = keep.tile([P, M], F32, name=f"result{b}")
-            nc.vector.tensor_tensor(result[:], acc[b][:], r_sb[b][:], ADD)
-            nc.sync.dma_start(out=out[b * P : (b + 1) * P, :], in_=result[:])
+                result = keep.tile([P, N_HALF], F32, name=f"result{b}{g}")
+                nc.vector.tensor_tensor(result[:], acc[b][g][:], r_sb[b][:, cols], ADD)
+                nc.sync.dma_start(out=out[b * P : (b + 1) * P, cols], in_=result[:])

@@ -26,6 +26,13 @@ def interleave(copy, out, src):
     copy(out=out.rearrange("p (c j) -> p c j", j=PACK), in_=src.rearrange("p j c -> p c j"))
 
 
+def interleave4(copy, out, src):
+    copy(
+        out=out.rearrange("p (c i j) -> p c j i", i=4, j=PACK),
+        in_=src.rearrange("p j (c i) -> p c j i", i=4),
+    )
+
+
 def tile_list_heads_tm_res_kernel(tc, xT, w, wgt, r, offs, out):
     nc = tc.nc
     with ExitStack() as ctx:
@@ -81,7 +88,7 @@ def tile_list_heads_tm_res_kernel(tc, xT, w, wgt, r, offs, out):
             w_codes = [keep.tile([P, N_HALF], U32, name=f"wcodes{a}{g}", align_bytes=64) for g in range(2)]
             w_scales = [keep.tile([P, N_HALF], U8, name=f"wscales{a}{g}", align_bytes=64) for g in range(2)]
             for g in range(2):
-                interleave(nc.scalar.copy if g else nc.vector.tensor_copy, w_bf[g][:], w_rows[:, :, g * N_HALF : (g + 1) * N_HALF])
+                interleave4(nc.scalar.copy if g else nc.vector.tensor_copy, w_bf[g][:], w_rows[:, :, g * N_HALF : (g + 1) * N_HALF])
             for g in range(2):
                 nc.vector.quantize_mx(out=w_codes[g][:].bitcast(FP8X4), scales=w_scales[g][:], in_=w_bf[g][:])
                 for b in range(S // P):
@@ -96,9 +103,13 @@ def tile_list_heads_tm_res_kernel(tc, xT, w, wgt, r, offs, out):
                         stop=a == PASSES - 1,
                     )
 
-        for g in range(2):
+        raw = keep.tile([P, N_HALF], F32, name="raw")
+        for b, g in ((0, 0), (1, 0), (2, 0), (0, 1), (3, 0), (1, 1), (2, 1), (3, 1)):
             cols = slice(g * N_HALF, (g + 1) * N_HALF)
-            for b in range(S // P):
-                result = keep.tile([P, N_HALF], F32, name=f"result{b}{g}")
+            result = keep.tile([P, N_HALF], F32, name=f"result{b}{g}")
+            if (b, g) == (3, 0):
+                nc.scalar.copy(out=raw[:], in_=acc[b][g][:])
+                nc.gpsimd.tensor_tensor(result[:], raw[:], r_sb[b][:, cols], ADD)
+            else:
                 nc.vector.tensor_tensor(result[:], acc[b][g][:], r_sb[b][:, cols], ADD)
-                nc.sync.dma_start(out=out[b * P : (b + 1) * P, cols], in_=result[:])
+            nc.sync.dma_start(out=out[b * P : (b + 1) * P, cols], in_=result[:])

from contextlib import ExitStack

import concourse.mybir as mybir

K, M, T, S = 1536, 512, 2048, 512
FLOPS = 2 * K * M * S

F32 = mybir.dt.float32
BF16 = mybir.dt.bfloat16
U32 = mybir.dt.uint32
U16 = mybir.dt.uint16
U8 = mybir.dt.uint8
FP8X4 = mybir.dt.float8_e4m3fn_x4
MULT = mybir.AluOpType.mult
ADD = mybir.AluOpType.add

P = 128
PACK = 4
K_PASS = P * PACK
PASSES = K // K_PASS
HALF = S // 2
N_HALF = M // 2


def interleave(copy, out, src):
    copy(out=out.rearrange("p (c j) -> p c j", j=PACK), in_=src.rearrange("p j c -> p c j"))


def interleave4(copy, out, src):
    copy(
        out=out.rearrange("p (c i j) -> p c j i", i=4, j=PACK),
        in_=src.rearrange("p j (c i) -> p c j i", i=4),
    )


def tile_list_heads_tm_res_kernel(tc, xT, w, wgt, r, offs, out):
    nc = tc.nc
    with ExitStack() as ctx:
        keep = ctx.enter_context(tc.tile_pool(name="keep", bufs=1))
        psum = ctx.enter_context(tc.psum_pool(name="psum", bufs=1))

        offsets = keep.tile([P, S // 16], U16, name="offsets")
        wgt_sb = keep.tile([P, S], F32, name="wgt_sb")
        x_sb = [[keep.tile([P, T], F32, name=f"x{a}{i}") for i in range(PACK)] for a in range(PASSES)]
        w_sb = [keep.tile([P, PACK * M], F32, name=f"w{a}") for a in range(PASSES)]
        r_sb = [keep.tile([P, M], F32, name=f"r{b}") for b in range(S // P)]

        for a in range(PASSES):
            x_rows = xT[a * K_PASS : (a + 1) * K_PASS, :].rearrange("(p j) t -> p j t", j=PACK)
            for i in range(PACK):
                queue = nc.scalar if i % 2 else nc.sync
                queue.dma_start(out=x_sb[a][i][:], in_=x_rows[:, i, :])
                if a == 0 and i == 0:
                    nc.sync.dma_start(offsets[:], offs)
                    nc.sync.dma_start(out=wgt_sb[:], in_=wgt)
        for a in range(PASSES):
            nc.sync.dma_start(
                out=w_sb[a][:],
                in_=w[a * K_PASS : (a + 1) * K_PASS, :].rearrange("(p j) n -> p (j n)", j=PACK),
            )
        for b in range(S // P):
            nc.sync.dma_start(out=r_sb[b][:], in_=r[b * P : (b + 1) * P, :])

        acc = [[psum.tile([P, N_HALF], F32, name=f"acc{b}{g}") for g in range(2)] for b in range(S // P)]
        x_codes = [[keep.tile([P, HALF], U32, name=f"xcodes{a}{h}", align_bytes=64) for h in range(2)] for a in range(PASSES)]
        x_scales = [[keep.tile([P, HALF], U8, name=f"xscales{a}{h}", align_bytes=64) for h in range(2)] for a in range(PASSES)]

        for a in range(PASSES):
            last = a == PASSES - 1
            picked = [keep.tile([P, PACK, HALF], F32, name=f"picked{a}{h}") for h in range(2)]
            x_bf = [keep.tile([P, HALF * PACK], BF16, name=f"xbf{a}{h}", align_bytes=64) for h in range(2)]
            for i in range(PACK):
                for h in range(2):
                    nc.vector.tensor_tensor(
                        picked[h][:, i, :],
                        x_sb[a][i][:].indirect(offsets[:, h * HALF // 16 : (h + 1) * HALF // 16]),
                        wgt_sb[:, h * HALF : (h + 1) * HALF],
                        MULT,
                    )
            interleave(nc.scalar.copy, x_bf[0][:], picked[0][:])
            interleave(nc.vector.tensor_copy if last else nc.scalar.copy, x_bf[1][:], picked[1][:])
            for h in range(2):
                nc.vector.quantize_mx(out=x_codes[a][h][:].bitcast(FP8X4), scales=x_scales[a][h][:], in_=x_bf[h][:])

        for a in range(PASSES):
            w_rows = w_sb[a][:].rearrange("p (j n) -> p j n", j=PACK)
            w_bf = [keep.tile([P, N_HALF * PACK], BF16, name=f"wbf{a}{g}", align_bytes=64) for g in range(2)]
            w_codes = [keep.tile([P, N_HALF], U32, name=f"wcodes{a}{g}", align_bytes=64) for g in range(2)]
            w_scales = [keep.tile([P, N_HALF], U8, name=f"wscales{a}{g}", align_bytes=64) for g in range(2)]
            for g in range(2):
                interleave4(nc.scalar.copy if g else nc.vector.tensor_copy, w_bf[g][:], w_rows[:, :, g * N_HALF : (g + 1) * N_HALF])
            for g in range(2):
                nc.vector.quantize_mx(out=w_codes[g][:].bitcast(FP8X4), scales=w_scales[g][:], in_=w_bf[g][:])
                for b in range(S // P):
                    h, cols = b // 2, slice(b % 2 * P, (b % 2 + 1) * P)
                    nc.tensor.matmul_mx(
                        out=acc[b][g][:],
                        lhsT=x_codes[a][h][:, cols].bitcast(FP8X4),
                        lhsT_scale=x_scales[a][h][:, cols],
                        rhs=w_codes[g][:].bitcast(FP8X4),
                        rhs_scale=w_scales[g][:],
                        start=a == 0,
                        stop=a == PASSES - 1,
                    )

        raw = keep.tile([P, N_HALF], F32, name="raw")
        for b, g in ((0, 0), (1, 0), (2, 0), (0, 1), (3, 0), (1, 1), (2, 1), (3, 1)):
            cols = slice(g * N_HALF, (g + 1) * N_HALF)
            result = keep.tile([P, N_HALF], F32, name=f"result{b}{g}")
            if (b, g) == (3, 0):
                nc.scalar.copy(out=raw[:], in_=acc[b][g][:])
                nc.gpsimd.tensor_tensor(result[:], raw[:], r_sb[b][:, cols], ADD)
            else:
                nc.vector.tensor_tensor(result[:], acc[b][g][:], r_sb[b][:, cols], ADD)
            nc.sync.dma_start(out=out[b * P : (b + 1) * P, cols], in_=result[:])
